import numpy as np
CORES = [87,215,343,471]
N = 4
ROOT = 1
WIDTHS = [40,3,17,120]
OFF = [0,40,43,60]
C = 180
def setup_inputs(rng):
    return {"x": rng.standard_normal((N, 128, C), dtype=np.float32)}
def reference(x):
    YW = max(WIDTHS)
    y = np.full((N, 128, YW), np.nan, x.dtype)
    for r in range(N):
        y[r][:, :WIDTHS[r]] = x[ROOT][:, OFF[r]:OFF[r] + WIDTHS[r]]
    return {"y": y}

@@ -1,0 +1,71 @@
+import concourse.bass as bass
+
+NP = 4
+W3 = 120 // NP
+
+SCRATCH = {
+    "d3": ("dram", [NP, 128, W3], "float32"),
+    "s": ("sbuf", [128, 60], "float32"),
+}
+SEMAPHORES = ["ld3", "ld", "st", "arr", "sent"]
+
+OFFCHIP = 8
+
+
+def relays(T):
+    c0, c2 = T.cores[0] - T.cores[0] % 8, T.cores[2] - T.cores[2] % 8
+    via0 = [c0 + 6, c0 + 4, c0 + 2, c0 + 0]
+    via2 = [c2 + 6, c2 + 2, c2 + 4, c2 + 0]
+    h = NP // 2
+    return via0[:h] + via2[:h]
+
+
+def rank_program(g, core, T, topo):
+    W, OFF = T.tables["WIDTHS"], T.tables["OFF"]
+    root, last = T.cores[1], T.cores[3]
+    rel = relays(T)
+    sem = T.sem
+    eng = OFFCHIP // NP
+
+    if core == root:
+        g.dma_start(out=T.d3[:], in_=T.x[:, OFF[3]:OFF[3] + W[3]]).then_inc(sem.ld3, 16)
+        g.dma_start(out=T.s[:], in_=T.x[:, 0:60]).then_inc(sem.ld, 16)
+        g.wait_ge(sem.ld3, 16)
+        trs = []
+        for k, r in enumerate(rel):
+            rid, pid = topo.addr(r, core)
+            trs.append(bass.RemoteDMATransfer(
+                dst_ids=[bass.DstId(rid=rid, pnc=pid)], dma_engine_mask=((1 << eng) - 1) << (k * eng),
+                remote_sem=sem.arr, src=T.d3[k], dst=T.d3[k]))
+        g.remote_dma_fused(trs, local_sem=sem.sent)
+        g.wait_ge(sem.ld, 16)
+        for q in (0, 2):
+            rid, pid = topo.addr(T.cores[q], core)
+            ap = T.s[:, OFF[q]:OFF[q] + W[q]]
+            g.remote_dma(out_ap=ap, in_ap=ap, remote_sem=sem.arr, local_sem=sem.sent, pid=pid, routing_id=rid,
+                         dma_engine_mask=0xFF)
+        g.dma_start(out=T.y[:, 0:W[1]], in_=T.x[:, OFF[1]:OFF[1] + W[1]]).then_inc(sem.st, 16)
+        g.wait_ge(sem.sent, 3 * OFFCHIP)
+        g.wait_ge(sem.st, 16)
+        return
+
+    if core in rel:
+        k = rel.index(core)
+        rid, pid = topo.addr(last, core)
+        g.wait_ge(sem.arr, eng)
+        g.remote_dma(out_ap=T.d3[k], in_ap=T.d3[k], remote_sem=sem.arr, local_sem=sem.sent, pid=pid, routing_id=rid,
+                     dma_engine_mask=0xFF)
+        g.wait_ge(sem.sent, OFFCHIP)
+        return
+
+    if core == last:
+        g.wait_ge(sem.arr, NP * OFFCHIP)
+        g.dma_start(out=T.y[:, :], in_=T.d3[:]).then_inc(sem.st, 16)
+        g.wait_ge(sem.st, 16)
+        return
+
+    q = T.rank_of(core)
+    if q is not None:
+        g.wait_ge(sem.arr, OFFCHIP)
+        g.dma_start(out=T.y[:, 0:W[q]], in_=T.s[:, OFF[q]:OFF[q] + W[q]]).then_inc(sem.st, 16)
+        g.wait_ge(sem.st, 16)

@@ -1,6 +1,7 @@
 import concourse.bass as bass
 
-NP = 4
+VIA0, VIA2 = 4, 2
+NP = VIA0 + VIA2
 W3 = 120 // NP
 
 SCRATCH = {
@@ -10,14 +11,15 @@ SCRATCH = {
 SEMAPHORES = ["ld3", "ld", "st", "arr", "sent"]
 
 OFFCHIP = 8
+MASKS = [0x01, 0x02, 0x04, 0x08, 0x30, 0xC0]
+ENGS = [1, 1, 1, 1, 2, 2]
 
 
 def relays(T):
     c0, c2 = T.cores[0] - T.cores[0] % 8, T.cores[2] - T.cores[2] % 8
     via0 = [c0 + 6, c0 + 4, c0 + 2, c0 + 0]
-    via2 = [c2 + 6, c2 + 2, c2 + 4, c2 + 0]
-    h = NP // 2
-    return via0[:h] + via2[:h]
+    via2 = [c2 + 6, c2 + 2]
+    return via0[:VIA0] + via2[:VIA2]
 
 
 def rank_program(g, core, T, topo):
@@ -25,7 +27,6 @@ def rank_program(g, core, T, topo):
     root, last = T.cores[1], T.cores[3]
     rel = relays(T)
     sem = T.sem
-    eng = OFFCHIP // NP
 
     if core == root:
         g.dma_start(out=T.d3[:], in_=T.x[:, OFF[3]:OFF[3] + W[3]]).then_inc(sem.ld3, 16)
@@ -35,7 +36,7 @@ def rank_program(g, core, T, topo):
         for k, r in enumerate(rel):
             rid, pid = topo.addr(r, core)
             trs.append(bass.RemoteDMATransfer(
-                dst_ids=[bass.DstId(rid=rid, pnc=pid)], dma_engine_mask=((1 << eng) - 1) << (k * eng),
+                dst_ids=[bass.DstId(rid=rid, pnc=pid)], dma_engine_mask=MASKS[k],
                 remote_sem=sem.arr, src=T.d3[k], dst=T.d3[k]))
         g.remote_dma_fused(trs, local_sem=sem.sent)
         g.wait_ge(sem.ld, 16)
@@ -52,7 +53,7 @@ def rank_program(g, core, T, topo):
     if core in rel:
         k = rel.index(core)
         rid, pid = topo.addr(last, core)
-        g.wait_ge(sem.arr, eng)
+        g.wait_ge(sem.arr, ENGS[k])
         g.remote_dma(out_ap=T.d3[k], in_ap=T.d3[k], remote_sem=sem.arr, local_sem=sem.sent, pid=pid, routing_id=rid,
                      dma_engine_mask=0xFF)
         g.wait_ge(sem.sent, OFFCHIP)

import concourse.bass as bass

VIA0, VIA2 = 4, 2
NP = VIA0 + VIA2
W3 = 120 // NP

SCRATCH = {
    "d3": ("dram", [NP, 128, W3], "float32"),
    "s": ("sbuf", [128, 60], "float32"),
}
SEMAPHORES = ["ld3", "ld", "st", "arr", "sent"]

OFFCHIP = 8
MASKS = [0x01, 0x02, 0x04, 0x08, 0x30, 0xC0]
ENGS = [1, 1, 1, 1, 2, 2]


def relays(T):
    c0, c2 = T.cores[0] - T.cores[0] % 8, T.cores[2] - T.cores[2] % 8
    via0 = [c0 + 6, c0 + 4, c0 + 2, c0 + 0]
    via2 = [c2 + 6, c2 + 2]
    return via0[:VIA0] + via2[:VIA2]


def rank_program(g, core, T, topo):
    W, OFF = T.tables["WIDTHS"], T.tables["OFF"]
    root, last = T.cores[1], T.cores[3]
    rel = relays(T)
    sem = T.sem

    if core == root:
        g.dma_start(out=T.d3[:], in_=T.x[:, OFF[3]:OFF[3] + W[3]]).then_inc(sem.ld3, 16)
        g.dma_start(out=T.s[:], in_=T.x[:, 0:60]).then_inc(sem.ld, 16)
        g.wait_ge(sem.ld3, 16)
        trs = []
        for k, r in enumerate(rel):
            rid, pid = topo.addr(r, core)
            trs.append(bass.RemoteDMATransfer(
                dst_ids=[bass.DstId(rid=rid, pnc=pid)], dma_engine_mask=MASKS[k],
                remote_sem=sem.arr, src=T.d3[k], dst=T.d3[k]))
        g.remote_dma_fused(trs, local_sem=sem.sent)
        g.wait_ge(sem.ld, 16)
        for q in (0, 2):
            rid, pid = topo.addr(T.cores[q], core)
            ap = T.s[:, OFF[q]:OFF[q] + W[q]]
            g.remote_dma(out_ap=ap, in_ap=ap, remote_sem=sem.arr, local_sem=sem.sent, pid=pid, routing_id=rid,
                         dma_engine_mask=0xFF)
        g.dma_start(out=T.y[:, 0:W[1]], in_=T.x[:, OFF[1]:OFF[1] + W[1]]).then_inc(sem.st, 16)
        g.wait_ge(sem.sent, 3 * OFFCHIP)
        g.wait_ge(sem.st, 16)
        return

    if core in rel:
        k = rel.index(core)
        rid, pid = topo.addr(last, core)
        g.wait_ge(sem.arr, ENGS[k])
        g.remote_dma(out_ap=T.d3[k], in_ap=T.d3[k], remote_sem=sem.arr, local_sem=sem.sent, pid=pid, routing_id=rid,
                     dma_engine_mask=0xFF)
        g.wait_ge(sem.sent, OFFCHIP)
        return

    if core == last:
        g.wait_ge(sem.arr, NP * OFFCHIP)
        g.dma_start(out=T.y[:, :], in_=T.d3[:]).then_inc(sem.st, 16)
        g.wait_ge(sem.st, 16)
        return

    q = T.rank_of(core)
    if q is not None:
        g.wait_ge(sem.arr, OFFCHIP)
        g.dma_start(out=T.y[:, 0:W[q]], in_=T.s[:, OFF[q]:OFF[q] + W[q]]).then_inc(sem.st, 16)
        g.wait_ge(sem.st, 16)
